import numpy as np
import ml_dtypes


def mxq(x, axis, fmt="e4m3"):
    dtype, down = {"e4m3": (ml_dtypes.float8_e4m3fn, 7), "e5m2": (ml_dtypes.float8_e5m2, 14)}[fmt]
    v = np.moveaxis(np.asarray(x, np.float32).astype(ml_dtypes.bfloat16).astype(np.float64), axis, -1)
    blocks = v.reshape(v.shape[:-1] + (-1, 32))
    amax = np.abs(blocks).max(-1, keepdims=True)
    byte = np.maximum(np.where(amax > 0, np.frexp(amax)[1] - 1 + 127, 0) - down, 1)
    scale = np.exp2(byte - 127.0)
    codes = (blocks / scale).astype(np.float32).astype(dtype).astype(np.float64)
    return np.moveaxis((codes * scale).reshape(v.shape), -1, axis)


WIDE = False


def mx_kscale(k):
    if not WIDE:
        return np.ones(k)
    levels = np.array([10, -10, 5, -5, 0])
    if k % 512:
        return np.exp2(np.random.permutation(np.resize(levels, k // 32))).repeat(32)
    a = np.empty((k // 512, 16))
    for p in range(k // 512):
        a[p, :8] = np.random.permutation(np.resize(levels, 8))
        for g in range(8):
            far = levels[np.abs(levels - a[p, g]) >= 10]
            a[p, g + 8] = far[np.random.randint(len(far))]
    return np.exp2(a.ravel()).repeat(32)


def f64(x):
    return np.asarray(x).astype(np.float64)


def striped(idx):
    return np.tile(idx.reshape(-1, 16).T, (8, 1)).astype(np.uint16)


def unstriped(offs):
    return offs[:16].T.reshape(-1).astype(np.int64)


def striped8(idx):
    return np.concatenate([x.reshape(-1, 16).T for x in idx]).astype(np.uint16)


def runs(offs, k):
    lists = np.stack([offs[16 * r : 16 * r + 16].T.reshape(-1) for r in range(8)]).astype(np.int64)
    return lists[np.arange(k) % 512 // 64]


def pack_weight(w):
    k, n = w.shape
    w = f64(np.asarray(w, np.float32).astype(ml_dtypes.bfloat16)).reshape(k // 32, 32, n)
    amax = np.abs(w).max(1)
    byte = np.clip(np.where(amax > 0, np.frexp(amax)[1] - 1 + 127 - 7, 1), 1, 254)
    scaled = (w * np.exp2(127.0 - byte)[:, None, :]).reshape(k, n).astype(np.float32)
    words = np.ascontiguousarray(scaled.reshape(k // 512, 128, 4, n).transpose(0, 1, 3, 2)).astype(ml_dtypes.float8_e4m3fn).view(np.uint8)
    return words, np.ascontiguousarray(byte.astype(np.uint8).reshape(k // 512, 16, n))


def unpack_weight(words, scales):
    g, p, n, _ = words.shape
    vals = np.ascontiguousarray(words).view(ml_dtypes.float8_e4m3fn).astype(np.float64) * np.repeat(np.exp2(scales.astype(np.float64) - 127.0), 8, axis=1)[..., None]
    return vals.transpose(0, 1, 3, 2).reshape(g * 512, n)


E2M1 = np.array([0.0, 0.5, 1.0, 1.5, 2.0, 3.0, 4.0, 6.0, -0.0, -0.5, -1.0, -1.5, -2.0, -3.0, -4.0, -6.0])


def pack_fp4(w):
    k, n = w.shape
    w = f64(np.asarray(w, np.float32).astype(ml_dtypes.bfloat16)).reshape(k // 32, 32, n)
    amax = np.abs(w).max(1)
    mant, ex = np.frexp(amax / 6.0)
    byte = np.clip(np.where(amax > 0, np.where(mant > 0.5, ex, ex - 1) + 127, 1), 1, 254)
    scaled = (w * np.exp2(127.0 - byte)[:, None, :]).reshape(k, n).astype(np.float32)
    c = np.ascontiguousarray(scaled.reshape(k // 512, 128, 4, n).transpose(0, 1, 3, 2)).astype(ml_dtypes.float4_e2m1fn).view(np.uint8) & 0xF
    words = (c[..., 0::2] | (c[..., 1::2] << 4)).reshape(k // 512, 128, 2 * n)
    return np.ascontiguousarray(words), np.ascontiguousarray(byte.astype(np.uint8).reshape(k // 512, 16, n))


def unpack_fp4(words, scales):
    g, _, n = scales.shape
    words = np.ascontiguousarray(words).reshape(g, 128, n, 2)
    nib = np.empty((g, 128, n, 4), np.uint8)
    nib[..., 0::2] = words & 0xF
    nib[..., 1::2] = words >> 4
    vals = E2M1[nib] * np.repeat(np.exp2(scales.astype(np.float64) - 127.0), 8, axis=1)[..., None]
    return vals.transpose(0, 1, 3, 2).reshape(g * 512, n)


def sigmoid(v):
    return 1.0 / (1.0 + np.exp(-np.maximum(v, -700.0)))

def planes(y):
    n, m = y.shape
    v = y.astype(np.float32).astype(ml_dtypes.bfloat16).astype(np.float64).reshape(n // 32, 32, m)
    top = np.abs(v).max(1)
    byte = np.clip(np.where(top > 0, np.frexp(top)[1] - 1 + 127 - 7, 1), 1, 254)
    codes = (v * np.exp2(127.0 - byte)[:, None, :]).reshape(n, m).astype(np.float32).astype(ml_dtypes.float8_e4m3fn).view(np.uint8)
    words = codes.reshape(n // 512, 128, 4, m).transpose(0, 1, 3, 2)
    return np.ascontiguousarray(words), np.ascontiguousarray(byte.astype(np.uint8).reshape(n // 512, 16, m))


K, T, S, N, H = 512, 2048, 512, 512, 512


def setup_inputs():
    n = np.random.standard_normal
    s = mx_kscale(K)[:, None]
    u = mx_kscale(H)
    packed_xT = pack_weight(n((K, T)) * s)
    packed_w1 = pack_fp4(n((K, H)) / np.sqrt(K) / s)
    packed_w2 = pack_fp4(n((H, N)) / np.sqrt(H) / u[:, None])
    return {
        "x_words": packed_xT[0],
        "x_scales": packed_xT[1],
        "w1_words": packed_w1[0],
        "w1_scales": packed_w1[1],
        "gn": (np.random.uniform(0.5, 1.5, (H, 1)) * u[:, None]).astype(np.float32),
        "w2_words": packed_w2[0],
        "w2_scales": packed_w2[1],
        "offs": striped(np.random.permutation(T)[:S]),
        "p1": striped8(np.stack([np.random.permutation(S) for _ in range(8)])),
        "p2": striped8(np.stack([np.random.permutation(S) for _ in range(8)])),
        "p3": striped8(np.stack([np.random.permutation(S) for _ in range(8)])),
    }


def reference(x_words, x_scales, w1_words, w1_scales, gn, w2_words, w2_scales, offs, p1, p2, p3):
    xq = unpack_weight(x_words, x_scales)[:, unstriped(offs)]
    y = np.tanh(unpack_fp4(w1_words, w1_scales).T @ xq)
    fl = y[np.arange(H)[:, None], runs(p1, H)] + y[np.arange(H)[:, None], runs(p2, H)] + y[np.arange(H)[:, None], runs(p3, H)]
    pr = sigmoid(-2.0 * (y * fl))
    z = f64(gn) * (y - (2.0 * (y * pr)))
    out_0 = unpack_fp4(w2_words, w2_scales).T @ mxq(z, 0, "e4m3")
    return (out_0,) + planes(out_0)

@@ -1,0 +1,232 @@
+from contextlib import ExitStack
+
+import concourse.mybir as mybir
+
+F32 = mybir.dt.float32
+BF16 = mybir.dt.bfloat16
+I32 = mybir.dt.int32
+U32 = mybir.dt.uint32
+U16 = mybir.dt.uint16
+U8 = mybir.dt.uint8
+FP8X4 = mybir.dt.float8_e4m3fn_x4
+FP4X4 = mybir.dt.float4_e2m1fn_x4
+ADD = mybir.AluOpType.add
+MULT = mybir.AluOpType.mult
+TANH = mybir.ActivationFunctionType.Tanh
+SIGMOID = mybir.ActivationFunctionType.Sigmoid
+COPY = mybir.ActivationFunctionType.Copy
+
+P = 128
+T, S = 2048, 512
+PACK = 4
+UNIT = 128
+CHUNKS = (256, 128, 128)
+ON_SCALAR = ((3, 0), (3, 1), (3, 2))
+FLOPS = 2 * 2 * 512 * 512 * 512
+
+
+def tile_picked_isingm_none_po_kernel(
+    tc, x_words, x_scales, w1_words, w1_scales, gn, w2_words, w2_scales, offs, p1, p2, p3, out_0, out_1, out_2
+):
+    nc = tc.nc
+    with ExitStack() as ctx:
+        keep = ctx.enter_context(tc.tile_pool(name="keep", bufs=1))
+        psum = ctx.enter_context(tc.psum_pool(name="psum", bufs=1))
+
+        def load_scale_rows(queue, tile, rows, quads=range(4)):
+            for q in quads:
+                queue.dma_start(out=tile[32 * q : 32 * q + 4, :].bitcast(I32), in_=rows[0, 4 * q : 4 * q + 4, :].bitcast(I32))
+
+        offs_t = keep.tile([P, S // 16], U16, name="offs_t")
+        lists = [keep.tile([P, S // 16], U16, name=f"list{k}") for k in range(3)]
+        xw = keep.tile([P, T], I32, name="xw", align_bytes=64)
+        xs = keep.tile([P, T], U8, name="xs", align_bytes=64)
+        w_raw = keep.tile([P, 2 * S], U8, name="w_raw", align_bytes=64)
+        ws_raw = keep.tile([P, S], U8, name="ws_raw", align_bytes=64)
+        w = [[keep.tile([P, 2 * P], U8, name=f"w{i}_{t}", align_bytes=64) for t in range(PACK)] for i in range(2)]
+        ws = [[keep.tile([P, P], U8, name=f"ws{i}_{t}", align_bytes=64) for t in range(PACK)] for i in range(2)]
+        gain = keep.tile([P, PACK], F32, name="gain")
+        warm = keep.tile([P, 1], F32, name="warm")
+        warm2 = keep.tile([P, 1], F32, name="warm2")
+
+        w2_raw = keep.tile([P, 2 * S], U8, name="w2_raw", align_bytes=64)
+        ws2_raw = keep.tile([P, S], U8, name="ws2_raw", align_bytes=64)
+        nc.vector.memset(xs[:].bitcast(I32), 0)
+        nc.vector.memset(ws_raw[:].bitcast(I32), 0)
+        nc.vector.memset(ws2_raw[:].bitcast(I32), 0)
+        nc.vector.memset(warm[:], 0.0)
+        nc.scalar.activation(warm2[:], warm[:], SIGMOID)
+
+        nc.sync.dma_start(offs_t[:], offs)
+        for k, src in enumerate((p1, p2, p3)):
+            nc.sync.dma_start(lists[k][:], src)
+        nc.sync.dma_start(out=w_raw[:].bitcast(I32), in_=w1_words[0].bitcast(I32))
+        nc.sync.dma_start(out=xw[:], in_=x_words[0].rearrange("p n t -> p (n t)").bitcast(I32))
+        load_scale_rows(nc.scalar, xs, x_scales)
+        load_scale_rows(nc.scalar, ws_raw, w1_scales)
+        load_scale_rows(nc.scalar, ws2_raw, w2_scales)
+        nc.gpsimd.dma_start(out=w2_raw[:].bitcast(I32), in_=w2_words[0].bitcast(I32))
+        nc.gpsimd.dma_start(out=gain[:], in_=gn.rearrange("(p t) o -> p (t o)", t=PACK))
+
+        def deal_words(i, t):
+            nc.vector.tensor_copy(
+                out=w[i][t][:].rearrange("p (m b) -> p m b", b=2),
+                in_=(w_raw, w2_raw)[i][:].rearrange("p (m t b) -> p t m b", t=PACK, b=2)[:, t],
+            )
+
+        def deal_scales(i, t):
+            nc.vector.tensor_copy(out=ws[i][t][:], in_=(ws_raw, ws2_raw)[i][:].rearrange("p (m t) -> p t m", t=PACK)[:, t])
+
+        gw = keep.tile([P, S], U32, name="gw", align_bytes=64)
+        gs = keep.tile([P, S], U8, name="gs", align_bytes=64)
+        for t in range(PACK):
+            deal_words(0, t)
+        nc.vector.tensor_copy(gs[:], xs[:].indirect(offs_t[:]))
+        nc.vector.tensor_copy(gw[:], xw[:].bitcast(U32).indirect(offs_t[:]))
+        for t in range(PACK):
+            deal_scales(0, t)
+
+        y = [keep.tile([P, S], F32, name=f"y{t}", align_bytes=64) for t in range(PACK)]
+        a = [keep.tile([P, S], F32, name=f"a{t}", align_bytes=64) for t in range(PACK)]
+        for t in range(PACK):
+            pre = psum.tile([P, S], F32, name=f"pre{t}")
+            nc.tensor.matmul_mx(
+                out=pre[:], lhsT=w[0][t][:].bitcast(FP4X4), lhsT_scale=ws[0][t][:],
+                rhs=gw[:].bitcast(FP8X4), rhs_scale=gs[:], start=True, stop=True,
+            )
+            nc.scalar.activation(y[t][:], pre[:], TANH)
+            if any(tt == t for tt, cc in ON_SCALAR):
+                nc.scalar.activation(a[t][:], pre[:], COPY)
+
+        out_rows = out_0.rearrange("(p t) j -> p t j", t=PACK)
+        out_words = out_1[0].rearrange("p n t -> p (n t)").bitcast(I32)
+        o_scales = keep.tile([P, S], U8, name="o_scales", align_bytes=64)
+        starts = [sum(CHUNKS[:c]) for c in range(len(CHUNKS))]
+        sig, yg, sums, us, ths, zq, obs = {}, {}, {}, {}, {}, {}, {}
+
+        def span(c):
+            return starts[c], CHUNKS[c]
+
+        def on_vector(c):
+            return [t for t in range(PACK) if (t, c) not in ON_SCALAR]
+
+        def on_scalar(c):
+            return [t for t in range(PACK) if (t, c) in ON_SCALAR]
+
+        def scalar_gathers(c):
+            c0, n = span(c)
+            for t in on_scalar(c):
+                for k in range(3):
+                    sig[c, t, k] = keep.tile([P, n], F32, name=f"sig{c}_{k}_{t}", align_bytes=64)
+                    nc.scalar.activation(sig[c, t, k][:], a[t][:].indirect(lists[k][:, c0 // 16 : (c0 + n) // 16]), SIGMOID, scale=2.0)
+
+        def gains(c):
+            c0, n = span(c)
+            yg[c] = keep.tile([P, PACK, n], F32, name=f"yg{c}", align_bytes=64)
+            for t in range(PACK):
+                nc.scalar.activation(yg[c][:, t, :], y[t][:, c0 : c0 + n], COPY, scale=gain[:, t : t + 1])
+
+        def vector_gathers(c, k):
+            c0, n = span(c)
+            tag = f"th{c - 1}" if (k == 1 and c > 0) else f"sum{c}_{k}"
+            sums[c, k] = keep.tile([P, PACK, n], F32, name=f"sum{c}_{k}", tag=tag, align_bytes=64)
+            picks = lists[k][:, c0 // 16 : (c0 + n) // 16]
+            for t in on_vector(c):
+                if k == 0:
+                    nc.vector.tensor_copy(sums[c, k][:, t, :], y[t][:].indirect(picks))
+                else:
+                    nc.vector.tensor_tensor(sums[c, k][:, t, :], y[t][:].indirect(picks), sums[c, k - 1][:, t, :], ADD)
+
+        def products(c):
+            c0, n = span(c)
+            mine, theirs = on_vector(c), on_scalar(c)
+            u = keep.tile([P, PACK, n], F32, name=f"u{c}", align_bytes=64)
+            two, half = {}, {}
+            for t in theirs:
+                two[t] = keep.tile([P, n], F32, name=f"two{c}_{t}", align_bytes=64)
+                nc.vector.tensor_tensor(two[t][:], sig[c, t, 0][:], sig[c, t, 1][:], ADD)
+            nc.vector.tensor_tensor(u[:, mine[0], :], sums[c, 2][:, mine[0], :], y[mine[0]][:, c0 : c0 + n], MULT)
+            for t in theirs:
+                half[t] = keep.tile([P, n], F32, name=f"half{c}_{t}", align_bytes=64)
+                nc.vector.scalar_tensor_tensor(half[t][:], sig[c, t, 2][:], -1.5, two[t][:], ADD, ADD)
+            for t in mine[1:]:
+                nc.vector.tensor_tensor(u[:, t, :], sums[c, 2][:, t, :], y[t][:, c0 : c0 + n], MULT)
+            for t in theirs:
+                nc.vector.scalar_tensor_tensor(u[:, t, :], half[t][:], 2.0, y[t][:, c0 : c0 + n], MULT, MULT)
+            us[c] = u
+
+        def flips(c):
+            c0, n = span(c)
+            ths[c] = keep.tile([P, PACK, n], F32, name=f"th{c}", tag=f"th{c}", align_bytes=64)
+            nc.scalar.activation(ths[c][:], us[c][:], TANH)
+
+        def quantise_z(c):
+            c0, n = span(c)
+            zb = keep.tile([P, n * PACK], BF16, name=f"zb{c}", align_bytes=64)
+            nc.vector.tensor_tensor(
+                zb[:].rearrange("p (c i t) -> p c t i", i=4, t=PACK),
+                ths[c][:].rearrange("p t (c i) -> p c t i", i=4),
+                yg[c][:].rearrange("p t (c i) -> p c t i", i=4),
+                MULT,
+            )
+            zw = keep.tile([P, n], U32, name=f"zw{c}", align_bytes=64)
+            zs = keep.tile([P, n], U8, name=f"zs{c}", align_bytes=64)
+            nc.vector.quantize_mx(out=zw[:].bitcast(FP8X4), scales=zs[:], in_=zb[:])
+            zq[c] = (zw, zs)
+
+        def second(c):
+            c0, n = span(c)
+            zw, zs = zq[c]
+            ob = keep.tile([P, n * PACK], BF16, name=f"ob{c}", align_bytes=64)
+            of = keep.tile([P, PACK, n], F32, name=f"of{c}", align_bytes=64)
+            last = c == len(CHUNKS) - 1
+            for u0 in range(0, n, UNIT):
+                acc = psum.tile([P, PACK, UNIT], F32, name=f"acc{(c0 + u0) // UNIT}")
+                for t in range(PACK):
+                    nc.tensor.matmul_mx(
+                        out=acc[:, t, :], lhsT=w[1][t][:].bitcast(FP4X4), lhsT_scale=ws[1][t][:],
+                        rhs=zw[:, u0 : u0 + UNIT].bitcast(FP8X4), rhs_scale=zs[:, u0 : u0 + UNIT], start=True, stop=True,
+                    )
+                words = ob[:, u0 * PACK : (u0 + UNIT) * PACK].rearrange("p (n t) -> p n t", t=PACK)
+                if last and True:
+                    nc.scalar.activation(of[:, :, u0 : u0 + UNIT], acc[:], COPY)
+                    nc.vector.tensor_copy(words, of[:, :, u0 : u0 + UNIT].rearrange("p t n -> p n t"))
+                else:
+                    nc.scalar.activation(words, acc[:].rearrange("p t n -> p n t"), COPY)
+                    nc.scalar.activation(of[:, :, u0 : u0 + UNIT], acc[:], COPY)
+            nc.sync.dma_start(out=out_rows[:, :, c0 : c0 + n], in_=of[:])
+            obs[c] = ob
+
+        def planes(c):
+            c0, n = span(c)
+            ow = keep.tile([P, n], I32, name=f"ow{c}", align_bytes=64)
+            nc.vector.quantize_mx(out=ow[:].bitcast(FP8X4), scales=o_scales[:, c0 : c0 + n], in_=obs[c][:])
+            nc.sync.dma_start(out=out_words[:, c0 : c0 + n], in_=ow[:])
+
+        last_c = len(CHUNKS) - 1
+        scalar_gathers(0)
+        gains(0)
+        for t in range(PACK):
+            deal_words(1, t)
+            deal_scales(1, t)
+        vector_gathers(0, 0)
+        for c in range(len(CHUNKS)):
+            vector_gathers(c, 1)
+            vector_gathers(c, 2)
+            products(c)
+            if c < last_c:
+                scalar_gathers(c + 1)
+                gains(c + 1)
+            if c > 0:
+                second(c - 1)
+            flips(c)
+            if c < last_c:
+                vector_gathers(c + 1, 0)
+            if c > 0:
+                planes(c - 1)
+            quantise_z(c)
+        second(last_c)
+        planes(last_c)
+
+        for q in range(4):
+            nc.sync.dma_start(out=out_2[0, 4 * q : 4 * q + 4, :].bitcast(I32), in_=o_scales[32 * q : 32 * q + 4, :].bitcast(I32))

@@ -20,8 +20,8 @@ P = 128
 T, S = 2048, 512
 PACK = 4
 UNIT = 128
+HALF = 256
 CHUNKS = (256, 128, 128)
-ON_SCALAR = ((3, 0), (3, 1), (3, 2))
 FLOPS = 2 * 2 * 512 * 512 * 512
 
 
@@ -41,132 +41,120 @@ def tile_picked_isingm_none_po_kernel(
         lists = [keep.tile([P, S // 16], U16, name=f"list{k}") for k in range(3)]
         xw = keep.tile([P, T], I32, name="xw", align_bytes=64)
         xs = keep.tile([P, T], U8, name="xs", align_bytes=64)
-        w_raw = keep.tile([P, 2 * S], U8, name="w_raw", align_bytes=64)
-        ws_raw = keep.tile([P, S], U8, name="ws_raw", align_bytes=64)
-        w = [[keep.tile([P, 2 * P], U8, name=f"w{i}_{t}", align_bytes=64) for t in range(PACK)] for i in range(2)]
-        ws = [[keep.tile([P, P], U8, name=f"ws{i}_{t}", align_bytes=64) for t in range(PACK)] for i in range(2)]
+        w_raw = [keep.tile([P, 2 * S], U8, name="w_raw", align_bytes=64)] * 2
+        ws_raw = [keep.tile([P, S], U8, name=f"ws_raw{i}", align_bytes=64) for i in range(2)]
+        w = [keep.tile([P, PACK, 2 * P], U8, name=f"w{i}", align_bytes=64) for i in range(2)]
+        ws = [keep.tile([P, PACK, P], U8, name=f"ws{i}", align_bytes=64) for i in range(2)]
         gain = keep.tile([P, PACK], F32, name="gain")
         warm = keep.tile([P, 1], F32, name="warm")
         warm2 = keep.tile([P, 1], F32, name="warm2")
 
-        w2_raw = keep.tile([P, 2 * S], U8, name="w2_raw", align_bytes=64)
-        ws2_raw = keep.tile([P, S], U8, name="ws2_raw", align_bytes=64)
         nc.vector.memset(xs[:].bitcast(I32), 0)
-        nc.vector.memset(ws_raw[:].bitcast(I32), 0)
-        nc.vector.memset(ws2_raw[:].bitcast(I32), 0)
+        nc.vector.memset(ws_raw[0][:].bitcast(I32), 0)
+        nc.vector.memset(ws_raw[1][:].bitcast(I32), 0)
         nc.vector.memset(warm[:], 0.0)
         nc.scalar.activation(warm2[:], warm[:], SIGMOID)
 
         nc.sync.dma_start(offs_t[:], offs)
         for k, src in enumerate((p1, p2, p3)):
             nc.sync.dma_start(lists[k][:], src)
-        nc.sync.dma_start(out=w_raw[:].bitcast(I32), in_=w1_words[0].bitcast(I32))
+        nc.sync.dma_start(out=w_raw[0][:].bitcast(I32), in_=w1_words[0].bitcast(I32))
         nc.sync.dma_start(out=xw[:], in_=x_words[0].rearrange("p n t -> p (n t)").bitcast(I32))
-        load_scale_rows(nc.scalar, xs, x_scales)
-        load_scale_rows(nc.scalar, ws_raw, w1_scales)
-        load_scale_rows(nc.scalar, ws2_raw, w2_scales)
-        nc.gpsimd.dma_start(out=w2_raw[:].bitcast(I32), in_=w2_words[0].bitcast(I32))
-        nc.gpsimd.dma_start(out=gain[:], in_=gn.rearrange("(p t) o -> p (t o)", t=PACK))
+        load_scale_rows(nc.sync, xs, x_scales)
+        load_scale_rows(nc.sync, ws_raw[0], w1_scales)
+        load_scale_rows(nc.sync, ws_raw[1], w2_scales)
 
-        def deal_words(i, t):
+        def deal_words(i):
             nc.vector.tensor_copy(
-                out=w[i][t][:].rearrange("p (m b) -> p m b", b=2),
-                in_=(w_raw, w2_raw)[i][:].rearrange("p (m t b) -> p t m b", t=PACK, b=2)[:, t],
+                out=w[i][:].rearrange("p t (m b) -> p t m b", b=2),
+                in_=w_raw[i][:].rearrange("p (m t b) -> p t m b", t=PACK, b=2),
             )
 
-        def deal_scales(i, t):
-            nc.vector.tensor_copy(out=ws[i][t][:], in_=(ws_raw, ws2_raw)[i][:].rearrange("p (m t) -> p t m", t=PACK)[:, t])
+        def deal_scales(i):
+            nc.vector.tensor_copy(out=ws[i][:], in_=ws_raw[i][:].rearrange("p (m t) -> p t m", t=PACK))
 
-        gw = keep.tile([P, S], U32, name="gw", align_bytes=64)
-        gs = keep.tile([P, S], U8, name="gs", align_bytes=64)
-        for t in range(PACK):
-            deal_words(0, t)
-        nc.vector.tensor_copy(gs[:], xs[:].indirect(offs_t[:]))
-        nc.vector.tensor_copy(gw[:], xw[:].bitcast(U32).indirect(offs_t[:]))
-        for t in range(PACK):
-            deal_scales(0, t)
+        gw = [keep.tile([P, HALF], U32, name=f"gw{h}", align_bytes=64) for h in range(2)]
+        gs = [keep.tile([P, HALF], U8, name=f"gs{h}", align_bytes=64) for h in range(2)]
+        deal_words(0)
+        nc.sync.dma_start(out=w_raw[1][:].bitcast(I32), in_=w2_words[0].bitcast(I32))
+        nc.gpsimd.dma_start(out=gain[:], in_=gn.rearrange("(p t) o -> p (t o)", t=PACK))
+        for h in range(2):
+            picks = offs_t[:, h * HALF // 16 : (h + 1) * HALF // 16]
+            nc.vector.tensor_copy(gw[h][:], xw[:].bitcast(U32).indirect(picks))
+            nc.vector.tensor_copy(gs[h][:], xs[:].indirect(picks))
+            if h == 0:
+                deal_scales(0)
+        deal_words(1)
+        deal_scales(1)
 
-        y = [keep.tile([P, S], F32, name=f"y{t}", align_bytes=64) for t in range(PACK)]
-        a = [keep.tile([P, S], F32, name=f"a{t}", align_bytes=64) for t in range(PACK)]
+        y = [keep.tile([P, S], F32, name=f"y{t}", align_bytes=64) for t in range(2)]
+        y_hi = keep.tile([P, 2, S], F32, name="y_hi", align_bytes=64)
+        a = [keep.tile([P, S], F32, name=f"a{t}", align_bytes=64) for t in range(2)]
+        yg = keep.tile([P, PACK, S], F32, name="yg", align_bytes=64)
+        for h in range(2):
+            cols = slice(h * HALF, (h + 1) * HALF)
+            for t in range(PACK):
+                pre = psum.tile([P, HALF], F32, name=f"pre{h}_{t}", tag=f"bank{4 * h + t}")
+                nc.tensor.matmul_mx(
+                    out=pre[:], lhsT=w[0][:, t, :].bitcast(FP4X4), lhsT_scale=ws[0][:, t, :],
+                    rhs=gw[h][:].bitcast(FP8X4), rhs_scale=gs[h][:], start=True, stop=True,
+                )
+                nc.scalar.activation(y[t][:, cols] if t < 2 else y_hi[:, t - 2, cols], pre[:], TANH)
+                if t >= 2:
+                    nc.scalar.activation(a[t - 2][:, cols], pre[:], COPY)
         for t in range(PACK):
-            pre = psum.tile([P, S], F32, name=f"pre{t}")
-            nc.tensor.matmul_mx(
-                out=pre[:], lhsT=w[0][t][:].bitcast(FP4X4), lhsT_scale=ws[0][t][:],
-                rhs=gw[:].bitcast(FP8X4), rhs_scale=gs[:], start=True, stop=True,
-            )
-            nc.scalar.activation(y[t][:], pre[:], TANH)
-            if any(tt == t for tt, cc in ON_SCALAR):
-                nc.scalar.activation(a[t][:], pre[:], COPY)
+            nc.gpsimd.tensor_scalar(yg[:, t, :], y[t][:] if t < 2 else y_hi[:, t - 2, :], gain[:, t : t + 1], 0.0, MULT, ADD)
 
         out_rows = out_0.rearrange("(p t) j -> p t j", t=PACK)
         out_words = out_1[0].rearrange("p n t -> p (n t)").bitcast(I32)
         o_scales = keep.tile([P, S], U8, name="o_scales", align_bytes=64)
         starts = [sum(CHUNKS[:c]) for c in range(len(CHUNKS))]
-        sig, yg, sums, us, ths, zq, obs = {}, {}, {}, {}, {}, {}, {}
+        sig, sums, us, ths, zq, obs = {}, {}, {}, {}, {}, {}
 
         def span(c):
             return starts[c], CHUNKS[c]
 
-        def on_vector(c):
-            return [t for t in range(PACK) if (t, c) not in ON_SCALAR]
-
-        def on_scalar(c):
-            return [t for t in range(PACK) if (t, c) in ON_SCALAR]
-
         def scalar_gathers(c):
             c0, n = span(c)
-            for t in on_scalar(c):
-                for k in range(3):
-                    sig[c, t, k] = keep.tile([P, n], F32, name=f"sig{c}_{k}_{t}", align_bytes=64)
-                    nc.scalar.activation(sig[c, t, k][:], a[t][:].indirect(lists[k][:, c0 // 16 : (c0 + n) // 16]), SIGMOID, scale=2.0)
+            for k in range(3):
+                sig[c, k] = keep.tile([P, 2, n], F32, name=f"sig{c}_{k}", align_bytes=64)
+                for t in range(2):
+                    nc.scalar.activation(sig[c, k][:, t, :], a[t][:].indirect(lists[k][:, c0 // 16 : (c0 + n) // 16]), SIGMOID, scale=2.0)
 
-        def gains(c):
-            c0, n = span(c)
-            yg[c] = keep.tile([P, PACK, n], F32, name=f"yg{c}", align_bytes=64)
-            for t in range(PACK):
-                nc.scalar.activation(yg[c][:, t, :], y[t][:, c0 : c0 + n], COPY, scale=gain[:, t : t + 1])
-
-        def vector_gathers(c, k):
-            c0, n = span(c)
-            tag = f"th{c - 1}" if (k == 1 and c > 0) else f"sum{c}_{k}"
-            sums[c, k] = keep.tile([P, PACK, n], F32, name=f"sum{c}_{k}", tag=tag, align_bytes=64)
-            picks = lists[k][:, c0 // 16 : (c0 + n) // 16]
-            for t in on_vector(c):
+        def vector_gathers(h, k):
+            picks = lists[k][:, h * HALF // 16 : (h + 1) * HALF // 16]
+            for t in range(2):
+                sums[h, k, t] = keep.tile([P, HALF], F32, name=f"sum{h}_{k}_{t}", align_bytes=64)
                 if k == 0:
-                    nc.vector.tensor_copy(sums[c, k][:, t, :], y[t][:].indirect(picks))
+                    nc.vector.tensor_copy(sums[h, k, t][:], y[t][:].indirect(picks))
                 else:
-                    nc.vector.tensor_tensor(sums[c, k][:, t, :], y[t][:].indirect(picks), sums[c, k - 1][:, t, :], ADD)
+                    nc.vector.tensor_tensor(sums[h, k, t][:], y[t][:].indirect(picks), sums[h, k - 1, t][:], ADD)
 
         def products(c):
             c0, n = span(c)
-            mine, theirs = on_vector(c), on_scalar(c)
+            h, r0 = divmod(c0, HALF)
             u = keep.tile([P, PACK, n], F32, name=f"u{c}", align_bytes=64)
-            two, half = {}, {}
-            for t in theirs:
-                two[t] = keep.tile([P, n], F32, name=f"two{c}_{t}", align_bytes=64)
-                nc.vector.tensor_tensor(two[t][:], sig[c, t, 0][:], sig[c, t, 1][:], ADD)
-            nc.vector.tensor_tensor(u[:, mine[0], :], sums[c, 2][:, mine[0], :], y[mine[0]][:, c0 : c0 + n], MULT)
-            for t in theirs:
-                half[t] = keep.tile([P, n], F32, name=f"half{c}_{t}", align_bytes=64)
-                nc.vector.scalar_tensor_tensor(half[t][:], sig[c, t, 2][:], -1.5, two[t][:], ADD, ADD)
-            for t in mine[1:]:
-                nc.vector.tensor_tensor(u[:, t, :], sums[c, 2][:, t, :], y[t][:, c0 : c0 + n], MULT)
-            for t in theirs:
-                nc.vector.scalar_tensor_tensor(u[:, t, :], half[t][:], 2.0, y[t][:, c0 : c0 + n], MULT, MULT)
+            two = keep.tile([P, 2, n], F32, name=f"two{c}", align_bytes=64)
+            half = keep.tile([P, 2, n], F32, name=f"half{c}", align_bytes=64)
+            nc.vector.tensor_tensor(two[:], sig[c, 0][:], sig[c, 1][:], ADD)
+            nc.vector.tensor_tensor(u[:, 0, :], sums[h, 2, 0][:, r0 : r0 + n], y[0][:, c0 : c0 + n], MULT)
+            nc.vector.scalar_tensor_tensor(half[:], sig[c, 2][:], -1.5, two[:], ADD, ADD)
+            nc.vector.tensor_tensor(u[:, 1, :], sums[h, 2, 1][:, r0 : r0 + n], y[1][:, c0 : c0 + n], MULT)
+            nc.vector.scalar_tensor_tensor(u[:, 2:4, :], half[:], 2.0, y_hi[:, :, c0 : c0 + n], MULT, MULT)
             us[c] = u
 
         def flips(c):
             c0, n = span(c)
-            ths[c] = keep.tile([P, PACK, n], F32, name=f"th{c}", tag=f"th{c}", align_bytes=64)
+            ths[c] = keep.tile([P, PACK, n], F32, name=f"th{c}", align_bytes=64)
             nc.scalar.activation(ths[c][:], us[c][:], TANH)
 
         def quantise_z(c):
             c0, n = span(c)
             zb = keep.tile([P, n * PACK], BF16, name=f"zb{c}", align_bytes=64)
             nc.vector.tensor_tensor(
-                zb[:].rearrange("p (c i t) -> p c t i", i=4, t=PACK),
-                ths[c][:].rearrange("p t (c i) -> p c t i", i=4),
-                yg[c][:].rearrange("p t (c i) -> p c t i", i=4),
+                zb[:].rearrange("p (c i t) -> p c t i", i=2, t=PACK),
+                ths[c][:].rearrange("p t (c i) -> p c t i", i=2),
+                yg[:, :, c0 : c0 + n].rearrange("p t (c i) -> p c t i", i=2),
                 MULT,
             )
             zw = keep.tile([P, n], U32, name=f"zw{c}", align_bytes=64)
@@ -178,23 +166,24 @@ def tile_picked_isingm_none_po_kernel(
             c0, n = span(c)
             zw, zs = zq[c]
             ob = keep.tile([P, n * PACK], BF16, name=f"ob{c}", align_bytes=64)
-            of = keep.tile([P, PACK, n], F32, name=f"of{c}", align_bytes=64)
-            last = c == len(CHUNKS) - 1
             for u0 in range(0, n, UNIT):
-                acc = psum.tile([P, PACK, UNIT], F32, name=f"acc{(c0 + u0) // UNIT}")
+                of = keep.tile([P, PACK, UNIT], F32, name=f"of{(c0 + u0) // UNIT}", align_bytes=64)
+                acc = psum.tile([P, PACK, UNIT], F32, name=f"acc{(c0 + u0) // UNIT}", tag=f"bank{(c0 + u0) // UNIT}")
                 for t in range(PACK):
                     nc.tensor.matmul_mx(
-                        out=acc[:, t, :], lhsT=w[1][t][:].bitcast(FP4X4), lhsT_scale=ws[1][t][:],
+                        out=acc[:, t, :], lhsT=w[1][:, t, :].bitcast(FP4X4), lhsT_scale=ws[1][:, t, :],
                         rhs=zw[:, u0 : u0 + UNIT].bitcast(FP8X4), rhs_scale=zs[:, u0 : u0 + UNIT], start=True, stop=True,
                     )
-                words = ob[:, u0 * PACK : (u0 + UNIT) * PACK].rearrange("p (n t) -> p n t", t=PACK)
-                if last and True:
-                    nc.scalar.activation(of[:, :, u0 : u0 + UNIT], acc[:], COPY)
-                    nc.vector.tensor_copy(words, of[:, :, u0 : u0 + UNIT].rearrange("p t n -> p n t"))
+                words = ob[:, u0 * PACK : (u0 + UNIT) * PACK]
+                if c in ():
+                    nc.scalar.activation(words.rearrange("p (n t) -> p n t", t=PACK), acc[:].rearrange("p t n -> p n t"), COPY)
+                    nc.scalar.activation(of[:], acc[:], COPY)
                 else:
-                    nc.scalar.activation(words, acc[:].rearrange("p t n -> p n t"), COPY)
-                    nc.scalar.activation(of[:, :, u0 : u0 + UNIT], acc[:], COPY)
-            nc.sync.dma_start(out=out_rows[:, :, c0 : c0 + n], in_=of[:])
+                    nc.scalar.activation(of[:], acc[:], COPY)
+                    nc.vector.tensor_copy(
+                        words.rearrange("p (c i t) -> p c t i", i=2, t=PACK), of[:].rearrange("p t (c i) -> p c t i", i=2)
+                    )
+                nc.sync.dma_start(out=out_rows[:, :, c0 + u0 : c0 + u0 + UNIT], in_=of[:])
             obs[c] = ob
 
         def planes(c):
@@ -203,30 +192,30 @@ def tile_picked_isingm_none_po_kernel(
             nc.vector.quantize_mx(out=ow[:].bitcast(FP8X4), scales=o_scales[:, c0 : c0 + n], in_=obs[c][:])
             nc.sync.dma_start(out=out_words[:, c0 : c0 + n], in_=ow[:])
 
-        last_c = len(CHUNKS) - 1
         scalar_gathers(0)
-        gains(0)
-        for t in range(PACK):
-            deal_words(1, t)
-            deal_scales(1, t)
         vector_gathers(0, 0)
-        for c in range(len(CHUNKS)):
-            vector_gathers(c, 1)
-            vector_gathers(c, 2)
-            products(c)
-            if c < last_c:
-                scalar_gathers(c + 1)
-                gains(c + 1)
-            if c > 0:
-                second(c - 1)
-            flips(c)
-            if c < last_c:
-                vector_gathers(c + 1, 0)
-            if c > 0:
-                planes(c - 1)
-            quantise_z(c)
-        second(last_c)
-        planes(last_c)
+        vector_gathers(1, 0)
+        vector_gathers(0, 1)
+        vector_gathers(0, 2)
+        products(0)
+        scalar_gathers(1)
+        vector_gathers(1, 1)
+        vector_gathers(1, 2)
+        flips(0)
+        scalar_gathers(2)
+        quantise_z(0)
+        products(1)
+        flips(1)
+        second(0)
+        products(2)
+        quantise_z(1)
+        flips(2)
+        planes(0)
+        second(1)
+        quantise_z(2)
+        planes(1)
+        second(2)
+        planes(2)
 
         for q in range(4):
-            nc.sync.dma_start(out=out_2[0, 4 * q : 4 * q + 4, :].bitcast(I32), in_=o_scales[32 * q : 32 * q + 4, :].bitcast(I32))
+            (nc.scalar, nc.sync)[q % 2].dma_start(out=out_2[0, 4 * q : 4 * q + 4, :].bitcast(I32), in_=o_scales[32 * q : 32 * q + 4, :].bitcast(I32))

@@ -49,8 +49,8 @@ def tile_picked_isingm_none_po_kernel(
         warm = keep.tile([P, 1], F32, name="warm")
         warm2 = keep.tile([P, 1], F32, name="warm2")
 
-        nc.vector.memset(xs[:].bitcast(I32), 0)
         nc.vector.memset(ws_raw[0][:].bitcast(I32), 0)
+        nc.vector.memset(xs[:].bitcast(I32), 0)
         nc.vector.memset(ws_raw[1][:].bitcast(I32), 0)
         nc.vector.memset(warm[:], 0.0)
         nc.scalar.activation(warm2[:], warm[:], SIGMOID)
@@ -58,10 +58,12 @@ def tile_picked_isingm_none_po_kernel(
         nc.sync.dma_start(offs_t[:], offs)
         for k, src in enumerate((p1, p2, p3)):
             nc.sync.dma_start(lists[k][:], src)
+        nc.sync.dma_start(out=gain[:], in_=gn.rearrange("(p t) o -> p (t o)", t=PACK))
         nc.sync.dma_start(out=w_raw[0][:].bitcast(I32), in_=w1_words[0].bitcast(I32))
         nc.sync.dma_start(out=xw[:], in_=x_words[0].rearrange("p n t -> p (n t)").bitcast(I32))
-        load_scale_rows(nc.sync, xs, x_scales)
+        load_scale_rows(nc.gpsimd, xs, x_scales, range(3, 4))
         load_scale_rows(nc.sync, ws_raw[0], w1_scales)
+        load_scale_rows(nc.sync, xs, x_scales, range(3))
         load_scale_rows(nc.sync, ws_raw[1], w2_scales)
 
         def deal_words(i):
@@ -73,17 +75,14 @@ def tile_picked_isingm_none_po_kernel(
         def deal_scales(i):
             nc.vector.tensor_copy(out=ws[i][:], in_=ws_raw[i][:].rearrange("p (m t) -> p t m", t=PACK))
 
-        gw = [keep.tile([P, HALF], U32, name=f"gw{h}", align_bytes=64) for h in range(2)]
-        gs = [keep.tile([P, HALF], U8, name=f"gs{h}", align_bytes=64) for h in range(2)]
+        gw = keep.tile([P, S], U32, name="gw", align_bytes=64)
+        gs = keep.tile([P, S], U8, name="gs", align_bytes=64)
         deal_words(0)
         nc.sync.dma_start(out=w_raw[1][:].bitcast(I32), in_=w2_words[0].bitcast(I32))
-        nc.gpsimd.dma_start(out=gain[:], in_=gn.rearrange("(p t) o -> p (t o)", t=PACK))
+        nc.vector.tensor_copy(gw[:], xw[:].bitcast(U32).indirect(offs_t[:]))
+        deal_scales(0)
         for h in range(2):
-            picks = offs_t[:, h * HALF // 16 : (h + 1) * HALF // 16]
-            nc.vector.tensor_copy(gw[h][:], xw[:].bitcast(U32).indirect(picks))
-            nc.vector.tensor_copy(gs[h][:], xs[:].indirect(picks))
-            if h == 0:
-                deal_scales(0)
+            nc.vector.tensor_copy(gs[:, h * HALF : (h + 1) * HALF], xs[:].indirect(offs_t[:, h * HALF // 16 : (h + 1) * HALF // 16]))
         deal_words(1)
         deal_scales(1)
 
@@ -91,19 +90,22 @@ def tile_picked_isingm_none_po_kernel(
         y_hi = keep.tile([P, 2, S], F32, name="y_hi", align_bytes=64)
         a = [keep.tile([P, S], F32, name=f"a{t}", align_bytes=64) for t in range(2)]
         yg = keep.tile([P, PACK, S], F32, name="yg", align_bytes=64)
+        def project(t, cols, scales, bank):
+            pre = psum.tile([P, cols.stop - cols.start], F32, name=f"pre{bank}", tag=f"bank{bank}")
+            nc.tensor.matmul_mx(
+                out=pre[:], lhsT=w[0][:, t, :].bitcast(FP4X4), lhsT_scale=ws[0][:, t, :],
+                rhs=gw[:, cols].bitcast(FP8X4), rhs_scale=scales, start=True, stop=True,
+            )
+            return pre
+
         for h in range(2):
             cols = slice(h * HALF, (h + 1) * HALF)
-            for t in range(PACK):
-                pre = psum.tile([P, HALF], F32, name=f"pre{h}_{t}", tag=f"bank{4 * h + t}")
-                nc.tensor.matmul_mx(
-                    out=pre[:], lhsT=w[0][:, t, :].bitcast(FP4X4), lhsT_scale=ws[0][:, t, :],
-                    rhs=gw[h][:].bitcast(FP8X4), rhs_scale=gs[h][:], start=True, stop=True,
-                )
-                nc.scalar.activation(y[t][:, cols] if t < 2 else y_hi[:, t - 2, cols], pre[:], TANH)
-                if t >= 2:
-                    nc.scalar.activation(a[t - 2][:, cols], pre[:], COPY)
-        for t in range(PACK):
-            nc.gpsimd.tensor_scalar(yg[:, t, :], y[t][:] if t < 2 else y_hi[:, t - 2, :], gain[:, t : t + 1], 0.0, MULT, ADD)
+            for t in range(2):
+                nc.scalar.activation(y[t][:, cols], project(t, cols, gs[:, cols], 2 * h + t)[:], TANH)
+        for t in range(2):
+            pre = project(2 + t, slice(0, S), gs[:], 4 + t)
+            nc.scalar.activation(a[t][:], pre[:], COPY)
+            nc.scalar.activation(y_hi[:, t, :], pre[:], TANH)
 
         out_rows = out_0.rearrange("(p t) j -> p t j", t=PACK)
         out_words = out_1[0].rearrange("p n t -> p (n t)").bitcast(I32)
@@ -114,12 +116,12 @@ def tile_picked_isingm_none_po_kernel(
         def span(c):
             return starts[c], CHUNKS[c]
 
-        def scalar_gathers(c):
-            c0, n = span(c)
+        def scalar_gathers(h):
             for k in range(3):
-                sig[c, k] = keep.tile([P, 2, n], F32, name=f"sig{c}_{k}", align_bytes=64)
+                sig[h, k] = keep.tile([P, 2, HALF], F32, name=f"sig{h}_{k}", align_bytes=64)
+                picks = lists[k][:, h * HALF // 16 : (h + 1) * HALF // 16]
                 for t in range(2):
-                    nc.scalar.activation(sig[c, k][:, t, :], a[t][:].indirect(lists[k][:, c0 // 16 : (c0 + n) // 16]), SIGMOID, scale=2.0)
+                    nc.scalar.activation(sig[h, k][:, t, :], a[t][:].indirect(picks), SIGMOID, scale=2.0)
 
         def vector_gathers(h, k):
             picks = lists[k][:, h * HALF // 16 : (h + 1) * HALF // 16]
@@ -136,12 +138,18 @@ def tile_picked_isingm_none_po_kernel(
             u = keep.tile([P, PACK, n], F32, name=f"u{c}", align_bytes=64)
             two = keep.tile([P, 2, n], F32, name=f"two{c}", align_bytes=64)
             half = keep.tile([P, 2, n], F32, name=f"half{c}", align_bytes=64)
-            nc.vector.tensor_tensor(two[:], sig[c, 0][:], sig[c, 1][:], ADD)
+            nc.vector.tensor_tensor(two[:], sig[h, 0][:, :, r0 : r0 + n], sig[h, 1][:, :, r0 : r0 + n], ADD)
             nc.vector.tensor_tensor(u[:, 0, :], sums[h, 2, 0][:, r0 : r0 + n], y[0][:, c0 : c0 + n], MULT)
-            nc.vector.scalar_tensor_tensor(half[:], sig[c, 2][:], -1.5, two[:], ADD, ADD)
+            nc.vector.scalar_tensor_tensor(half[:], sig[h, 2][:, :, r0 : r0 + n], -1.5, two[:], ADD, ADD)
             nc.vector.tensor_tensor(u[:, 1, :], sums[h, 2, 1][:, r0 : r0 + n], y[1][:, c0 : c0 + n], MULT)
             nc.vector.scalar_tensor_tensor(u[:, 2:4, :], half[:], 2.0, y_hi[:, :, c0 : c0 + n], MULT, MULT)
             us[c] = u
+
+        def gains(c):
+            c0, n = span(c)
+            for t in range(PACK):
+                spins = y[t][:, c0 : c0 + n] if t < 2 else y_hi[:, t - 2, c0 : c0 + n]
+                nc.scalar.activation(yg[:, t, c0 : c0 + n], spins, COPY, scale=gain[:, t : t + 1])
 
         def flips(c):
             c0, n = span(c)
@@ -201,13 +209,15 @@ def tile_picked_isingm_none_po_kernel(
         scalar_gathers(1)
         vector_gathers(1, 1)
         vector_gathers(1, 2)
+        gains(0)
         flips(0)
-        scalar_gathers(2)
         quantise_z(0)
         products(1)
+        gains(1)
         flips(1)
-        second(0)
         products(2)
+        gains(2)
+        second(0)
         quantise_z(1)
         flips(2)
         planes(0)

@@ -17,12 +17,18 @@ SIGMOID = mybir.ActivationFunctionType.Sigmoid
 COPY = mybir.ActivationFunctionType.Copy
 
 P = 128
-T, S = 2048, 512
+T = 2048
+S = 512
 PACK = 4
-UNIT = 128
-HALF = 256
+SHARE = 2
+LISTS = 3
+GROUP = 16
+QUADS = 4
+HALF = S // 2
 CHUNKS = (256, 128, 128)
-FLOPS = 2 * 2 * 512 * 512 * 512
+NARROW = min(CHUNKS)
+PAIR = 2
+FLOPS = 2 * (2 * S * S * S)
 
 
 def tile_picked_isingm_none_po_kernel(
@@ -33,199 +39,198 @@ def tile_picked_isingm_none_po_kernel(
         keep = ctx.enter_context(tc.tile_pool(name="keep", bufs=1))
         psum = ctx.enter_context(tc.psum_pool(name="psum", bufs=1))
 
-        def load_scale_rows(queue, tile, rows, quads=range(4)):
+        def load_scale_rows(queue, tile, rows, quads):
             for q in quads:
-                queue.dma_start(out=tile[32 * q : 32 * q + 4, :].bitcast(I32), in_=rows[0, 4 * q : 4 * q + 4, :].bitcast(I32))
+                queue.dma_start(
+                    out=tile[32 * q : 32 * q + 4, :].bitcast(I32), in_=rows[0, 4 * q : 4 * q + 4, :].bitcast(I32)
+                )
 
-        offs_t = keep.tile([P, S // 16], U16, name="offs_t")
-        lists = [keep.tile([P, S // 16], U16, name=f"list{k}") for k in range(3)]
-        xw = keep.tile([P, T], I32, name="xw", align_bytes=64)
-        xs = keep.tile([P, T], U8, name="xs", align_bytes=64)
-        w_raw = [keep.tile([P, 2 * S], U8, name="w_raw", align_bytes=64)] * 2
-        ws_raw = [keep.tile([P, S], U8, name=f"ws_raw{i}", align_bytes=64) for i in range(2)]
-        w = [keep.tile([P, PACK, 2 * P], U8, name=f"w{i}", align_bytes=64) for i in range(2)]
-        ws = [keep.tile([P, PACK, P], U8, name=f"ws{i}", align_bytes=64) for i in range(2)]
+        def entries(list_tile, h):
+            return list_tile[:, h * HALF // GROUP : (h + 1) * HALF // GROUP]
+
+        def interleaved(tile):
+            return tile.rearrange("p (c i t) -> p c t i", i=PAIR, t=PACK)
+
+        def by_pairs(planes_view):
+            return planes_view.rearrange("p t (c i) -> p c t i", i=PAIR)
+
+        picks = keep.tile([P, S // GROUP], U16, name="picks")
+        neighbours = [keep.tile([P, S // GROUP], U16, name=f"neighbours{k}") for k in range(LISTS)]
+        x_codes = keep.tile([P, T], I32, name="x_codes", align_bytes=64)
+        x_bytes = keep.tile([P, T], U8, name="x_bytes", align_bytes=64)
+        w_codes_raw = [keep.tile([P, 2 * S], U8, name=f"w_codes_raw{i}", align_bytes=64) for i in range(2)]
+        w_bytes_raw = [keep.tile([P, S], U8, name=f"w_bytes_raw{i}", align_bytes=64) for i in range(2)]
+        w_codes = [keep.tile([P, PACK, 2 * P], U8, name=f"w_codes{i}", align_bytes=64) for i in range(2)]
+        w_bytes = [keep.tile([P, PACK, P], U8, name=f"w_bytes{i}", align_bytes=64) for i in range(2)]
         gain = keep.tile([P, PACK], F32, name="gain")
-        warm = keep.tile([P, 1], F32, name="warm")
-        warm2 = keep.tile([P, 1], F32, name="warm2")
+        warm_in = keep.tile([P, 1], F32, name="warm_in")
+        warm_out = keep.tile([P, 1], F32, name="warm_out")
 
-        nc.vector.memset(ws_raw[0][:].bitcast(I32), 0)
-        nc.vector.memset(xs[:].bitcast(I32), 0)
-        nc.vector.memset(ws_raw[1][:].bitcast(I32), 0)
-        nc.vector.memset(warm[:], 0.0)
-        nc.scalar.activation(warm2[:], warm[:], SIGMOID)
+        nc.vector.memset(w_bytes_raw[0][:].bitcast(I32), 0)
+        nc.vector.memset(x_bytes[:].bitcast(I32), 0)
+        nc.vector.memset(w_bytes_raw[1][:].bitcast(I32), 0)
+        nc.vector.memset(warm_in[:], 0.0)
+        nc.scalar.activation(warm_out[:], warm_in[:], SIGMOID)
 
-        nc.sync.dma_start(offs_t[:], offs)
-        for k, src in enumerate((p1, p2, p3)):
-            nc.sync.dma_start(lists[k][:], src)
+        nc.sync.dma_start(picks[:], offs)
+        for tile, source in zip(neighbours, (p1, p2, p3)):
+            nc.sync.dma_start(tile[:], source)
         nc.sync.dma_start(out=gain[:], in_=gn.rearrange("(p t) o -> p (t o)", t=PACK))
-        nc.sync.dma_start(out=w_raw[0][:].bitcast(I32), in_=w1_words[0].bitcast(I32))
-        nc.sync.dma_start(out=xw[:], in_=x_words[0].rearrange("p n t -> p (n t)").bitcast(I32))
-        load_scale_rows(nc.gpsimd, xs, x_scales, range(3, 4))
-        load_scale_rows(nc.sync, ws_raw[0], w1_scales)
-        load_scale_rows(nc.sync, xs, x_scales, range(3))
-        load_scale_rows(nc.sync, ws_raw[1], w2_scales)
+        nc.sync.dma_start(out=w_codes_raw[0][:].bitcast(I32), in_=w1_words[0].bitcast(I32))
+        nc.sync.dma_start(out=w_codes_raw[1][:].bitcast(I32), in_=w2_words[0].bitcast(I32))
+        nc.sync.dma_start(out=x_codes[:], in_=x_words[0].rearrange("p n t -> p (n t)").bitcast(I32))
+        load_scale_rows(nc.gpsimd, x_bytes, x_scales, range(QUADS - 1, QUADS))
+        load_scale_rows(nc.sync, w_bytes_raw[0], w1_scales, range(QUADS))
+        load_scale_rows(nc.sync, x_bytes, x_scales, range(QUADS - 1))
+        load_scale_rows(nc.sync, w_bytes_raw[1], w2_scales, range(QUADS))
 
-        def deal_words(i):
+        def deal_codes(i):
             nc.vector.tensor_copy(
-                out=w[i][:].rearrange("p t (m b) -> p t m b", b=2),
-                in_=w_raw[i][:].rearrange("p (m t b) -> p t m b", t=PACK, b=2),
+                out=w_codes[i][:].rearrange("p t (m b) -> p t m b", b=2),
+                in_=w_codes_raw[i][:].rearrange("p (m t b) -> p t m b", t=PACK, b=2),
             )
 
-        def deal_scales(i):
-            nc.vector.tensor_copy(out=ws[i][:], in_=ws_raw[i][:].rearrange("p (m t) -> p t m", t=PACK))
+        def deal_bytes(i):
+            nc.vector.tensor_copy(out=w_bytes[i][:], in_=w_bytes_raw[i][:].rearrange("p (m t) -> p t m", t=PACK))
 
-        gw = keep.tile([P, S], U32, name="gw", align_bytes=64)
-        gs = keep.tile([P, S], U8, name="gs", align_bytes=64)
-        deal_words(0)
-        nc.sync.dma_start(out=w_raw[1][:].bitcast(I32), in_=w2_words[0].bitcast(I32))
-        nc.vector.tensor_copy(gw[:], xw[:].bitcast(U32).indirect(offs_t[:]))
-        deal_scales(0)
-        for h in range(2):
-            nc.vector.tensor_copy(gs[:, h * HALF : (h + 1) * HALF], xs[:].indirect(offs_t[:, h * HALF // 16 : (h + 1) * HALF // 16]))
-        deal_words(1)
-        deal_scales(1)
-
-        y = [keep.tile([P, S], F32, name=f"y{t}", align_bytes=64) for t in range(2)]
-        y_hi = keep.tile([P, 2, S], F32, name="y_hi", align_bytes=64)
-        a = [keep.tile([P, S], F32, name=f"a{t}", align_bytes=64) for t in range(2)]
-        yg = keep.tile([P, PACK, S], F32, name="yg", align_bytes=64)
-        def project(t, cols, scales, bank):
-            pre = psum.tile([P, cols.stop - cols.start], F32, name=f"pre{bank}", tag=f"bank{bank}")
+        def product(acc, i, t, codes, scales):
             nc.tensor.matmul_mx(
-                out=pre[:], lhsT=w[0][:, t, :].bitcast(FP4X4), lhsT_scale=ws[0][:, t, :],
-                rhs=gw[:, cols].bitcast(FP8X4), rhs_scale=scales, start=True, stop=True,
+                out=acc, lhsT=w_codes[i][:, t, :].bitcast(FP4X4), lhsT_scale=w_bytes[i][:, t, :],
+                rhs=codes.bitcast(FP8X4), rhs_scale=scales, start=True, stop=True,
             )
-            return pre
+
+        picked_codes = keep.tile([P, S], U32, name="picked_codes", align_bytes=64)
+        picked_bytes = keep.tile([P, S], U8, name="picked_bytes", align_bytes=64)
+        deal_codes(0)
+        deal_codes(1)
+        nc.vector.tensor_copy(picked_codes[:], x_codes[:].bitcast(U32).indirect(picks[:]))
+        deal_bytes(0)
+        for h in range(2):
+            nc.vector.tensor_copy(picked_bytes[:, h * HALF : (h + 1) * HALF], x_bytes[:].indirect(entries(picks, h)))
+        deal_bytes(1)
+
+        y_low = [keep.tile([P, S], F32, name=f"y_low{t}", align_bytes=64) for t in range(SHARE)]
+        y_high = keep.tile([P, SHARE, S], F32, name="y_high", align_bytes=64)
+        a_high = [keep.tile([P, S], F32, name=f"a_high{t}", align_bytes=64) for t in range(SHARE)]
+        gained = keep.tile([P, PACK, S], F32, name="gained", align_bytes=64)
+
+        def first_product(t, cols, bank):
+            acc = psum.tile([P, cols.stop - cols.start], F32, name=f"first{bank}", tag=f"bank{bank}")
+            product(acc[:], 0, t, picked_codes[:, cols], picked_bytes[:, cols])
+            return acc
 
         for h in range(2):
             cols = slice(h * HALF, (h + 1) * HALF)
-            for t in range(2):
-                nc.scalar.activation(y[t][:, cols], project(t, cols, gs[:, cols], 2 * h + t)[:], TANH)
-        for t in range(2):
-            pre = project(2 + t, slice(0, S), gs[:], 4 + t)
-            nc.scalar.activation(a[t][:], pre[:], COPY)
-            nc.scalar.activation(y_hi[:, t, :], pre[:], TANH)
+            for t in range(SHARE):
+                nc.scalar.activation(y_low[t][:, cols], first_product(t, cols, SHARE * h + t)[:], TANH)
+        for t in range(SHARE):
+            acc = first_product(SHARE + t, slice(0, S), 2 * SHARE + t)
+            nc.scalar.activation(a_high[t][:], acc[:], COPY)
+            nc.scalar.activation(y_high[:, t, :], acc[:], TANH)
 
         out_rows = out_0.rearrange("(p t) j -> p t j", t=PACK)
-        out_words = out_1[0].rearrange("p n t -> p (n t)").bitcast(I32)
-        o_scales = keep.tile([P, S], U8, name="o_scales", align_bytes=64)
+        out_codes = out_1[0].rearrange("p n t -> p (n t)").bitcast(I32)
+        result_bytes = keep.tile([P, S], U8, name="result_bytes", align_bytes=64)
         starts = [sum(CHUNKS[:c]) for c in range(len(CHUNKS))]
-        sig, sums, us, ths, zq, obs = {}, {}, {}, {}, {}, {}
-
-        def span(c):
-            return starts[c], CHUNKS[c]
+        sigmoids, sums, energy, flip, z_packed, result_bf16 = {}, {}, {}, {}, {}, {}
 
         def scalar_gathers(h):
-            for k in range(3):
-                sig[h, k] = keep.tile([P, 2, HALF], F32, name=f"sig{h}_{k}", align_bytes=64)
-                picks = lists[k][:, h * HALF // 16 : (h + 1) * HALF // 16]
-                for t in range(2):
-                    nc.scalar.activation(sig[h, k][:, t, :], a[t][:].indirect(picks), SIGMOID, scale=2.0)
+            for k in range(LISTS):
+                sigmoids[h, k] = keep.tile([P, SHARE, HALF], F32, name=f"sigmoids{h}_{k}", align_bytes=64)
+                for t in range(SHARE):
+                    nc.scalar.activation(
+                        sigmoids[h, k][:, t, :], a_high[t][:].indirect(entries(neighbours[k], h)), SIGMOID, scale=2.0
+                    )
 
         def vector_gathers(h, k):
-            picks = lists[k][:, h * HALF // 16 : (h + 1) * HALF // 16]
-            for t in range(2):
-                sums[h, k, t] = keep.tile([P, HALF], F32, name=f"sum{h}_{k}_{t}", align_bytes=64)
+            for t in range(SHARE):
+                sums[h, k, t] = keep.tile([P, HALF], F32, name=f"sums{h}_{k}_{t}", align_bytes=64)
+                looked_up = y_low[t][:].indirect(entries(neighbours[k], h))
                 if k == 0:
-                    nc.vector.tensor_copy(sums[h, k, t][:], y[t][:].indirect(picks))
+                    nc.vector.tensor_copy(sums[h, k, t][:], looked_up)
                 else:
-                    nc.vector.tensor_tensor(sums[h, k, t][:], y[t][:].indirect(picks), sums[h, k - 1, t][:], ADD)
+                    nc.vector.tensor_tensor(sums[h, k, t][:], looked_up, sums[h, k - 1, t][:], ADD)
 
-        def products(c):
-            c0, n = span(c)
+        def energies(c):
+            c0, n = starts[c], CHUNKS[c]
             h, r0 = divmod(c0, HALF)
-            u = keep.tile([P, PACK, n], F32, name=f"u{c}", align_bytes=64)
-            two = keep.tile([P, 2, n], F32, name=f"two{c}", align_bytes=64)
-            half = keep.tile([P, 2, n], F32, name=f"half{c}", align_bytes=64)
-            nc.vector.tensor_tensor(two[:], sig[h, 0][:, :, r0 : r0 + n], sig[h, 1][:, :, r0 : r0 + n], ADD)
-            nc.vector.tensor_tensor(u[:, 0, :], sums[h, 2, 0][:, r0 : r0 + n], y[0][:, c0 : c0 + n], MULT)
-            nc.vector.scalar_tensor_tensor(half[:], sig[h, 2][:, :, r0 : r0 + n], -1.5, two[:], ADD, ADD)
-            nc.vector.tensor_tensor(u[:, 1, :], sums[h, 2, 1][:, r0 : r0 + n], y[1][:, c0 : c0 + n], MULT)
-            nc.vector.scalar_tensor_tensor(u[:, 2:4, :], half[:], 2.0, y_hi[:, :, c0 : c0 + n], MULT, MULT)
-            us[c] = u
+            within = slice(r0, r0 + n)
+            energy[c] = keep.tile([P, PACK, n], F32, name=f"energy{c}", align_bytes=64)
+            two = keep.tile([P, SHARE, n], F32, name=f"two{c}", align_bytes=64)
+            half_field = keep.tile([P, SHARE, n], F32, name=f"half_field{c}", align_bytes=64)
+            nc.vector.tensor_tensor(two[:], sigmoids[h, 0][:, :, within], sigmoids[h, 1][:, :, within], ADD)
+            nc.vector.tensor_tensor(energy[c][:, 0, :], sums[h, 2, 0][:, within], y_low[0][:, c0 : c0 + n], MULT)
+            nc.vector.scalar_tensor_tensor(half_field[:], sigmoids[h, 2][:, :, within], -1.5, two[:], ADD, ADD)
+            nc.vector.tensor_tensor(energy[c][:, 1, :], sums[h, 2, 1][:, within], y_low[1][:, c0 : c0 + n], MULT)
+            nc.vector.scalar_tensor_tensor(
+                energy[c][:, SHARE:PACK, :], half_field[:], 2.0, y_high[:, :, c0 : c0 + n], MULT, MULT
+            )
 
         def gains(c):
-            c0, n = span(c)
+            cols = slice(starts[c], starts[c] + CHUNKS[c])
             for t in range(PACK):
-                spins = y[t][:, c0 : c0 + n] if t < 2 else y_hi[:, t - 2, c0 : c0 + n]
-                nc.scalar.activation(yg[:, t, c0 : c0 + n], spins, COPY, scale=gain[:, t : t + 1])
+                spins = y_low[t][:, cols] if t < SHARE else y_high[:, t - SHARE, cols]
+                nc.scalar.activation(gained[:, t, cols], spins, COPY, scale=gain[:, t : t + 1])
 
         def flips(c):
-            c0, n = span(c)
-            ths[c] = keep.tile([P, PACK, n], F32, name=f"th{c}", align_bytes=64)
-            nc.scalar.activation(ths[c][:], us[c][:], TANH)
+            flip[c] = keep.tile([P, PACK, CHUNKS[c]], F32, name=f"flip{c}", align_bytes=64)
+            nc.scalar.activation(flip[c][:], energy[c][:], TANH)
 
         def quantise_z(c):
-            c0, n = span(c)
-            zb = keep.tile([P, n * PACK], BF16, name=f"zb{c}", align_bytes=64)
+            c0, n = starts[c], CHUNKS[c]
+            z_bf16 = keep.tile([P, n * PACK], BF16, name=f"z_bf16_{c}", align_bytes=64)
             nc.vector.tensor_tensor(
-                zb[:].rearrange("p (c i t) -> p c t i", i=2, t=PACK),
-                ths[c][:].rearrange("p t (c i) -> p c t i", i=2),
-                yg[:, :, c0 : c0 + n].rearrange("p t (c i) -> p c t i", i=2),
-                MULT,
+                interleaved(z_bf16[:]), by_pairs(flip[c][:]), by_pairs(gained[:, :, c0 : c0 + n]), MULT
             )
-            zw = keep.tile([P, n], U32, name=f"zw{c}", align_bytes=64)
-            zs = keep.tile([P, n], U8, name=f"zs{c}", align_bytes=64)
-            nc.vector.quantize_mx(out=zw[:].bitcast(FP8X4), scales=zs[:], in_=zb[:])
-            zq[c] = (zw, zs)
+            z_codes = keep.tile([P, n], U32, name=f"z_codes{c}", align_bytes=64)
+            z_bytes = keep.tile([P, n], U8, name=f"z_bytes{c}", align_bytes=64)
+            nc.vector.quantize_mx(out=z_codes[:].bitcast(FP8X4), scales=z_bytes[:], in_=z_bf16[:])
+            z_packed[c] = (z_codes, z_bytes)
 
-        def second(c):
-            c0, n = span(c)
-            zw, zs = zq[c]
-            ob = keep.tile([P, n * PACK], BF16, name=f"ob{c}", align_bytes=64)
-            for u0 in range(0, n, UNIT):
-                of = keep.tile([P, PACK, UNIT], F32, name=f"of{(c0 + u0) // UNIT}", align_bytes=64)
-                acc = psum.tile([P, PACK, UNIT], F32, name=f"acc{(c0 + u0) // UNIT}", tag=f"bank{(c0 + u0) // UNIT}")
-                for t in range(PACK):
-                    nc.tensor.matmul_mx(
-                        out=acc[:, t, :], lhsT=w[1][:, t, :].bitcast(FP4X4), lhsT_scale=ws[1][:, t, :],
-                        rhs=zw[:, u0 : u0 + UNIT].bitcast(FP8X4), rhs_scale=zs[:, u0 : u0 + UNIT], start=True, stop=True,
-                    )
-                words = ob[:, u0 * PACK : (u0 + UNIT) * PACK]
-                if c in ():
-                    nc.scalar.activation(words.rearrange("p (n t) -> p n t", t=PACK), acc[:].rearrange("p t n -> p n t"), COPY)
-                    nc.scalar.activation(of[:], acc[:], COPY)
-                else:
-                    nc.scalar.activation(of[:], acc[:], COPY)
-                    nc.vector.tensor_copy(
-                        words.rearrange("p (c i t) -> p c t i", i=2, t=PACK), of[:].rearrange("p t (c i) -> p c t i", i=2)
-                    )
-                nc.sync.dma_start(out=out_rows[:, :, c0 + u0 : c0 + u0 + UNIT], in_=of[:])
-            obs[c] = ob
+        def second_product(c):
+            c0, n = starts[c], CHUNKS[c]
+            z_codes, z_bytes = z_packed[c]
+            result_bf16[c] = keep.tile([P, n * PACK], BF16, name=f"result_bf16_{c}", align_bytes=64)
+            result = keep.tile([P, PACK, n], F32, name=f"result{c}", align_bytes=64)
+            per_bank = S // n
+            for t0 in range(0, PACK, per_bank):
+                bank = c0 // NARROW + t0 // per_bank
+                acc = psum.tile([P, per_bank, n], F32, name=f"second{bank}", tag=f"bank{bank}")
+                for t in range(per_bank):
+                    product(acc[:, t, :], 1, t0 + t, z_codes[:], z_bytes[:])
+                rows = slice(t0, t0 + per_bank)
+                nc.scalar.activation(result[:, rows, :], acc[:], COPY)
+                nc.sync.dma_start(out=out_rows[:, rows, c0 : c0 + n], in_=result[:, rows, :])
+            nc.vector.tensor_copy(interleaved(result_bf16[c][:]), by_pairs(result[:]))
 
-        def planes(c):
-            c0, n = span(c)
-            ow = keep.tile([P, n], I32, name=f"ow{c}", align_bytes=64)
-            nc.vector.quantize_mx(out=ow[:].bitcast(FP8X4), scales=o_scales[:, c0 : c0 + n], in_=obs[c][:])
-            nc.sync.dma_start(out=out_words[:, c0 : c0 + n], in_=ow[:])
+        def quantise_result(c):
+            c0, n = starts[c], CHUNKS[c]
+            result_codes = keep.tile([P, n], I32, name=f"result_codes{c}", align_bytes=64)
+            nc.vector.quantize_mx(
+                out=result_codes[:].bitcast(FP8X4), scales=result_bytes[:, c0 : c0 + n], in_=result_bf16[c][:]
+            )
+            nc.sync.dma_start(out=out_codes[:, c0 : c0 + n], in_=result_codes[:])
 
-        scalar_gathers(0)
-        vector_gathers(0, 0)
-        vector_gathers(1, 0)
-        vector_gathers(0, 1)
-        vector_gathers(0, 2)
-        products(0)
-        scalar_gathers(1)
-        vector_gathers(1, 1)
-        vector_gathers(1, 2)
-        gains(0)
-        flips(0)
-        quantise_z(0)
-        products(1)
-        gains(1)
-        flips(1)
-        products(2)
-        gains(2)
-        second(0)
-        quantise_z(1)
-        flips(2)
-        planes(0)
-        second(1)
-        quantise_z(2)
-        planes(1)
-        second(2)
-        planes(2)
-
-        for q in range(4):
-            (nc.scalar, nc.sync)[q % 2].dma_start(out=out_2[0, 4 * q : 4 * q + 4, :].bitcast(I32), in_=o_scales[32 * q : 32 * q + 4, :].bitcast(I32))
+        for h in range(2):
+            scalar_gathers(h)
+            for k in range(LISTS):
+                vector_gathers(h, k)
+        last = len(CHUNKS) - 1
+        energies(0)
+        for c in range(len(CHUNKS)):
+            gains(c)
+            flips(c)
+            if c < last:
+                energies(c + 1)
+            quantise_z(c)
+            if c > 0:
+                second_product(c - 1)
+            if c > 1:
+                quantise_result(c - 2)
+        second_product(last)
+        quantise_result(last - 1)
+        quantise_result(last)
+        for q in range(QUADS):
+            (nc.scalar, nc.sync)[q % 2].dma_start(
+                out=out_2[0, 4 * q : 4 * q + 4, :].bitcast(I32), in_=result_bytes[32 * q : 32 * q + 4, :].bitcast(I32)
+            )

@@ -25,8 +25,7 @@ LISTS = 3
 GROUP = 16
 QUADS = 4
 HALF = S // 2
-CHUNKS = (256, 128, 128)
-NARROW = min(CHUNKS)
+CHUNK = 128
 PAIR = 2
 FLOPS = 2 * (2 * S * S * S)
 
@@ -131,7 +130,6 @@ def tile_picked_isingm_none_po_kernel(
         out_rows = out_0.rearrange("(p t) j -> p t j", t=PACK)
         out_codes = out_1[0].rearrange("p n t -> p (n t)").bitcast(I32)
         result_bytes = keep.tile([P, S], U8, name="result_bytes", align_bytes=64)
-        starts = [sum(CHUNKS[:c]) for c in range(len(CHUNKS))]
         sigmoids, sums, energy, flip, z_packed, result_bf16 = {}, {}, {}, {}, {}, {}
 
         def scalar_gathers(h):
@@ -151,85 +149,76 @@ def tile_picked_isingm_none_po_kernel(
                 else:
                     nc.vector.tensor_tensor(sums[h, k, t][:], looked_up, sums[h, k - 1, t][:], ADD)
 
-        def energies(c):
-            c0, n = starts[c], CHUNKS[c]
-            h, r0 = divmod(c0, HALF)
-            within = slice(r0, r0 + n)
-            energy[c] = keep.tile([P, PACK, n], F32, name=f"energy{c}", align_bytes=64)
-            two = keep.tile([P, SHARE, n], F32, name=f"two{c}", align_bytes=64)
-            half_field = keep.tile([P, SHARE, n], F32, name=f"half_field{c}", align_bytes=64)
-            nc.vector.tensor_tensor(two[:], sigmoids[h, 0][:, :, within], sigmoids[h, 1][:, :, within], ADD)
-            nc.vector.tensor_tensor(energy[c][:, 0, :], sums[h, 2, 0][:, within], y_low[0][:, c0 : c0 + n], MULT)
-            nc.vector.scalar_tensor_tensor(half_field[:], sigmoids[h, 2][:, :, within], -1.5, two[:], ADD, ADD)
-            nc.vector.tensor_tensor(energy[c][:, 1, :], sums[h, 2, 1][:, within], y_low[1][:, c0 : c0 + n], MULT)
+        def energies(h):
+            cols = slice(h * HALF, (h + 1) * HALF)
+            energy[h] = keep.tile([P, PACK, HALF], F32, name=f"energy{h}", align_bytes=64)
+            two = keep.tile([P, SHARE, HALF], F32, name=f"two{h}", align_bytes=64)
+            half_field = keep.tile([P, SHARE, HALF], F32, name=f"half_field{h}", align_bytes=64)
+            nc.vector.tensor_tensor(two[:], sigmoids[h, 0][:], sigmoids[h, 1][:], ADD)
+            nc.vector.tensor_tensor(energy[h][:, 0, :], sums[h, 2, 0][:], y_low[0][:, cols], MULT)
+            nc.vector.scalar_tensor_tensor(half_field[:], sigmoids[h, 2][:], -1.5, two[:], ADD, ADD)
+            nc.vector.tensor_tensor(energy[h][:, 1, :], sums[h, 2, 1][:], y_low[1][:, cols], MULT)
             nc.vector.scalar_tensor_tensor(
-                energy[c][:, SHARE:PACK, :], half_field[:], 2.0, y_high[:, :, c0 : c0 + n], MULT, MULT
+                energy[h][:, SHARE:PACK, :], half_field[:], 2.0, y_high[:, :, cols], MULT, MULT
             )
 
-        def gains(c):
-            cols = slice(starts[c], starts[c] + CHUNKS[c])
+        def gains(h):
+            cols = slice(h * HALF, (h + 1) * HALF)
             for t in range(PACK):
                 spins = y_low[t][:, cols] if t < SHARE else y_high[:, t - SHARE, cols]
                 nc.scalar.activation(gained[:, t, cols], spins, COPY, scale=gain[:, t : t + 1])
 
         def flips(c):
-            flip[c] = keep.tile([P, PACK, CHUNKS[c]], F32, name=f"flip{c}", align_bytes=64)
-            nc.scalar.activation(flip[c][:], energy[c][:], TANH)
+            h, r0 = divmod(c * CHUNK, HALF)
+            flip[c] = keep.tile([P, PACK, CHUNK], F32, name=f"flip{c}", align_bytes=64)
+            nc.scalar.activation(flip[c][:], energy[h][:, :, r0 : r0 + CHUNK], TANH)
 
         def quantise_z(c):
-            c0, n = starts[c], CHUNKS[c]
-            z_bf16 = keep.tile([P, n * PACK], BF16, name=f"z_bf16_{c}", align_bytes=64)
-            nc.vector.tensor_tensor(
-                interleaved(z_bf16[:]), by_pairs(flip[c][:]), by_pairs(gained[:, :, c0 : c0 + n]), MULT
-            )
-            z_codes = keep.tile([P, n], U32, name=f"z_codes{c}", align_bytes=64)
-            z_bytes = keep.tile([P, n], U8, name=f"z_bytes{c}", align_bytes=64)
+            cols = slice(c * CHUNK, (c + 1) * CHUNK)
+            z_bf16 = keep.tile([P, CHUNK * PACK], BF16, name=f"z_bf16_{c}", align_bytes=64)
+            nc.vector.tensor_tensor(interleaved(z_bf16[:]), by_pairs(flip[c][:]), by_pairs(gained[:, :, cols]), MULT)
+            z_codes = keep.tile([P, CHUNK], U32, name=f"z_codes{c}", align_bytes=64)
+            z_bytes = keep.tile([P, CHUNK], U8, name=f"z_bytes{c}", align_bytes=64)
             nc.vector.quantize_mx(out=z_codes[:].bitcast(FP8X4), scales=z_bytes[:], in_=z_bf16[:])
             z_packed[c] = (z_codes, z_bytes)
 
         def second_product(c):
-            c0, n = starts[c], CHUNKS[c]
             z_codes, z_bytes = z_packed[c]
-            result_bf16[c] = keep.tile([P, n * PACK], BF16, name=f"result_bf16_{c}", align_bytes=64)
-            result = keep.tile([P, PACK, n], F32, name=f"result{c}", align_bytes=64)
-            per_bank = S // n
-            for t0 in range(0, PACK, per_bank):
-                bank = c0 // NARROW + t0 // per_bank
-                acc = psum.tile([P, per_bank, n], F32, name=f"second{bank}", tag=f"bank{bank}")
-                for t in range(per_bank):
-                    product(acc[:, t, :], 1, t0 + t, z_codes[:], z_bytes[:])
-                rows = slice(t0, t0 + per_bank)
-                nc.scalar.activation(result[:, rows, :], acc[:], COPY)
-                nc.sync.dma_start(out=out_rows[:, rows, c0 : c0 + n], in_=result[:, rows, :])
+            acc = psum.tile([P, PACK, CHUNK], F32, name=f"second{c}", tag=f"bank{c}")
+            for t in range(PACK):
+                product(acc[:, t, :], 1, t, z_codes[:], z_bytes[:])
+            result = keep.tile([P, PACK, CHUNK], F32, name=f"result{c}", align_bytes=64)
+            nc.scalar.activation(result[:], acc[:], COPY)
+            nc.sync.dma_start(out=out_rows[:, :, c * CHUNK : (c + 1) * CHUNK], in_=result[:])
+            result_bf16[c] = keep.tile([P, CHUNK * PACK], BF16, name=f"result_bf16_{c}", align_bytes=64)
             nc.vector.tensor_copy(interleaved(result_bf16[c][:]), by_pairs(result[:]))
 
         def quantise_result(c):
-            c0, n = starts[c], CHUNKS[c]
-            result_codes = keep.tile([P, n], I32, name=f"result_codes{c}", align_bytes=64)
+            cols = slice(c * CHUNK, (c + 1) * CHUNK)
+            result_codes = keep.tile([P, CHUNK], I32, name=f"result_codes{c}", align_bytes=64)
             nc.vector.quantize_mx(
-                out=result_codes[:].bitcast(FP8X4), scales=result_bytes[:, c0 : c0 + n], in_=result_bf16[c][:]
+                out=result_codes[:].bitcast(FP8X4), scales=result_bytes[:, cols], in_=result_bf16[c][:]
             )
-            nc.sync.dma_start(out=out_codes[:, c0 : c0 + n], in_=result_codes[:])
+            nc.sync.dma_start(out=out_codes[:, cols], in_=result_codes[:])
 
+        per_half = HALF // CHUNK
         for h in range(2):
             scalar_gathers(h)
             for k in range(LISTS):
                 vector_gathers(h, k)
-        last = len(CHUNKS) - 1
         energies(0)
-        for c in range(len(CHUNKS)):
-            gains(c)
-            flips(c)
-            if c < last:
-                energies(c + 1)
-            quantise_z(c)
-            if c > 0:
-                second_product(c - 1)
-            if c > 1:
-                quantise_result(c - 2)
-        second_product(last)
-        quantise_result(last - 1)
-        quantise_result(last)
+        for h in range(2):
+            gains(h)
+            for c in range(h * per_half, (h + 1) * per_half):
+                flips(c)
+            if h == 0:
+                energies(1)
+            for c in range(h * per_half, (h + 1) * per_half):
+                quantise_z(c)
+        for c in range(S // CHUNK):
+            second_product(c)
+        for c in range(S // CHUNK):
+            quantise_result(c)
         for q in range(QUADS):
             (nc.scalar, nc.sync)[q % 2].dma_start(
                 out=out_2[0, 4 * q : 4 * q + 4, :].bitcast(I32), in_=result_bytes[32 * q : 32 * q + 4, :].bitcast(I32)

from contextlib import ExitStack

import concourse.mybir as mybir

F32 = mybir.dt.float32
BF16 = mybir.dt.bfloat16
I32 = mybir.dt.int32
U32 = mybir.dt.uint32
U16 = mybir.dt.uint16
U8 = mybir.dt.uint8
FP8X4 = mybir.dt.float8_e4m3fn_x4
FP4X4 = mybir.dt.float4_e2m1fn_x4
ADD = mybir.AluOpType.add
MULT = mybir.AluOpType.mult
TANH = mybir.ActivationFunctionType.Tanh
SIGMOID = mybir.ActivationFunctionType.Sigmoid
COPY = mybir.ActivationFunctionType.Copy

P = 128
T = 2048
S = 512
PACK = 4
SHARE = 2
LISTS = 3
GROUP = 16
QUADS = 4
HALF = S // 2
CHUNK = 128
PAIR = 2
FLOPS = 2 * (2 * S * S * S)


def tile_picked_isingm_none_po_kernel(
    tc, x_words, x_scales, w1_words, w1_scales, gn, w2_words, w2_scales, offs, p1, p2, p3, out_0, out_1, out_2
):
    nc = tc.nc
    with ExitStack() as ctx:
        keep = ctx.enter_context(tc.tile_pool(name="keep", bufs=1))
        psum = ctx.enter_context(tc.psum_pool(name="psum", bufs=1))

        def load_scale_rows(queue, tile, rows, quads):
            for q in quads:
                queue.dma_start(
                    out=tile[32 * q : 32 * q + 4, :].bitcast(I32), in_=rows[0, 4 * q : 4 * q + 4, :].bitcast(I32)
                )

        def entries(list_tile, h):
            return list_tile[:, h * HALF // GROUP : (h + 1) * HALF // GROUP]

        def interleaved(tile):
            return tile.rearrange("p (c i t) -> p c t i", i=PAIR, t=PACK)

        def by_pairs(planes_view):
            return planes_view.rearrange("p t (c i) -> p c t i", i=PAIR)

        picks = keep.tile([P, S // GROUP], U16, name="picks")
        neighbours = [keep.tile([P, S // GROUP], U16, name=f"neighbours{k}") for k in range(LISTS)]
        x_codes = keep.tile([P, T], I32, name="x_codes", align_bytes=64)
        x_bytes = keep.tile([P, T], U8, name="x_bytes", align_bytes=64)
        w_codes_raw = [keep.tile([P, 2 * S], U8, name=f"w_codes_raw{i}", align_bytes=64) for i in range(2)]
        w_bytes_raw = [keep.tile([P, S], U8, name=f"w_bytes_raw{i}", align_bytes=64) for i in range(2)]
        w_codes = [keep.tile([P, PACK, 2 * P], U8, name=f"w_codes{i}", align_bytes=64) for i in range(2)]
        w_bytes = [keep.tile([P, PACK, P], U8, name=f"w_bytes{i}", align_bytes=64) for i in range(2)]
        gain = keep.tile([P, PACK], F32, name="gain")
        warm_in = keep.tile([P, 1], F32, name="warm_in")
        warm_out = keep.tile([P, 1], F32, name="warm_out")

        nc.vector.memset(w_bytes_raw[0][:].bitcast(I32), 0)
        nc.vector.memset(x_bytes[:].bitcast(I32), 0)
        nc.vector.memset(w_bytes_raw[1][:].bitcast(I32), 0)
        nc.vector.memset(warm_in[:], 0.0)
        nc.scalar.activation(warm_out[:], warm_in[:], SIGMOID)

        nc.sync.dma_start(picks[:], offs)
        for tile, source in zip(neighbours, (p1, p2, p3)):
            nc.sync.dma_start(tile[:], source)
        nc.sync.dma_start(out=gain[:], in_=gn.rearrange("(p t) o -> p (t o)", t=PACK))
        nc.sync.dma_start(out=w_codes_raw[0][:].bitcast(I32), in_=w1_words[0].bitcast(I32))
        nc.sync.dma_start(out=w_codes_raw[1][:].bitcast(I32), in_=w2_words[0].bitcast(I32))
        nc.sync.dma_start(out=x_codes[:], in_=x_words[0].rearrange("p n t -> p (n t)").bitcast(I32))
        load_scale_rows(nc.gpsimd, x_bytes, x_scales, range(QUADS - 1, QUADS))
        load_scale_rows(nc.sync, w_bytes_raw[0], w1_scales, range(QUADS))
        load_scale_rows(nc.sync, x_bytes, x_scales, range(QUADS - 1))
        load_scale_rows(nc.sync, w_bytes_raw[1], w2_scales, range(QUADS))

        def deal_codes(i):
            nc.vector.tensor_copy(
                out=w_codes[i][:].rearrange("p t (m b) -> p t m b", b=2),
                in_=w_codes_raw[i][:].rearrange("p (m t b) -> p t m b", t=PACK, b=2),
            )

        def deal_bytes(i):
            nc.vector.tensor_copy(out=w_bytes[i][:], in_=w_bytes_raw[i][:].rearrange("p (m t) -> p t m", t=PACK))

        def product(acc, i, t, codes, scales):
            nc.tensor.matmul_mx(
                out=acc, lhsT=w_codes[i][:, t, :].bitcast(FP4X4), lhsT_scale=w_bytes[i][:, t, :],
                rhs=codes.bitcast(FP8X4), rhs_scale=scales, start=True, stop=True,
            )

        picked_codes = keep.tile([P, S], U32, name="picked_codes", align_bytes=64)
        picked_bytes = keep.tile([P, S], U8, name="picked_bytes", align_bytes=64)
        deal_codes(0)
        deal_codes(1)
        nc.vector.tensor_copy(picked_codes[:], x_codes[:].bitcast(U32).indirect(picks[:]))
        deal_bytes(0)
        for h in range(2):
            nc.vector.tensor_copy(picked_bytes[:, h * HALF : (h + 1) * HALF], x_bytes[:].indirect(entries(picks, h)))
        deal_bytes(1)

        y_low = [keep.tile([P, S], F32, name=f"y_low{t}", align_bytes=64) for t in range(SHARE)]
        y_high = keep.tile([P, SHARE, S], F32, name="y_high", align_bytes=64)
        a_high = [keep.tile([P, S], F32, name=f"a_high{t}", align_bytes=64) for t in range(SHARE)]
        gained = keep.tile([P, PACK, S], F32, name="gained", align_bytes=64)

        def first_product(t, cols, bank):
            acc = psum.tile([P, cols.stop - cols.start], F32, name=f"first{bank}", tag=f"bank{bank}")
            product(acc[:], 0, t, picked_codes[:, cols], picked_bytes[:, cols])
            return acc

        for h in range(2):
            cols = slice(h * HALF, (h + 1) * HALF)
            for t in range(SHARE):
                nc.scalar.activation(y_low[t][:, cols], first_product(t, cols, SHARE * h + t)[:], TANH)
        for t in range(SHARE):
            acc = first_product(SHARE + t, slice(0, S), 2 * SHARE + t)
            nc.scalar.activation(a_high[t][:], acc[:], COPY)
            nc.scalar.activation(y_high[:, t, :], acc[:], TANH)

        out_rows = out_0.rearrange("(p t) j -> p t j", t=PACK)
        out_codes = out_1[0].rearrange("p n t -> p (n t)").bitcast(I32)
        result_bytes = keep.tile([P, S], U8, name="result_bytes", align_bytes=64)
        sigmoids, sums, energy, flip, z_packed, result_bf16 = {}, {}, {}, {}, {}, {}

        def scalar_gathers(h):
            for k in range(LISTS):
                sigmoids[h, k] = keep.tile([P, SHARE, HALF], F32, name=f"sigmoids{h}_{k}", align_bytes=64)
                for t in range(SHARE):
                    nc.scalar.activation(
                        sigmoids[h, k][:, t, :], a_high[t][:].indirect(entries(neighbours[k], h)), SIGMOID, scale=2.0
                    )

        def vector_gathers(h, k):
            for t in range(SHARE):
                sums[h, k, t] = keep.tile([P, HALF], F32, name=f"sums{h}_{k}_{t}", align_bytes=64)
                looked_up = y_low[t][:].indirect(entries(neighbours[k], h))
                if k == 0:
                    nc.vector.tensor_copy(sums[h, k, t][:], looked_up)
                else:
                    nc.vector.tensor_tensor(sums[h, k, t][:], looked_up, sums[h, k - 1, t][:], ADD)

        def energies(h):
            cols = slice(h * HALF, (h + 1) * HALF)
            energy[h] = keep.tile([P, PACK, HALF], F32, name=f"energy{h}", align_bytes=64)
            two = keep.tile([P, SHARE, HALF], F32, name=f"two{h}", align_bytes=64)
            half_field = keep.tile([P, SHARE, HALF], F32, name=f"half_field{h}", align_bytes=64)
            nc.vector.tensor_tensor(two[:], sigmoids[h, 0][:], sigmoids[h, 1][:], ADD)
            nc.vector.tensor_tensor(energy[h][:, 0, :], sums[h, 2, 0][:], y_low[0][:, cols], MULT)
            nc.vector.scalar_tensor_tensor(half_field[:], sigmoids[h, 2][:], -1.5, two[:], ADD, ADD)
            nc.vector.tensor_tensor(energy[h][:, 1, :], sums[h, 2, 1][:], y_low[1][:, cols], MULT)
            nc.vector.scalar_tensor_tensor(
                energy[h][:, SHARE:PACK, :], half_field[:], 2.0, y_high[:, :, cols], MULT, MULT
            )

        def gains(h):
            cols = slice(h * HALF, (h + 1) * HALF)
            for t in range(PACK):
                spins = y_low[t][:, cols] if t < SHARE else y_high[:, t - SHARE, cols]
                nc.scalar.activation(gained[:, t, cols], spins, COPY, scale=gain[:, t : t + 1])

        def flips(c):
            h, r0 = divmod(c * CHUNK, HALF)
            flip[c] = keep.tile([P, PACK, CHUNK], F32, name=f"flip{c}", align_bytes=64)
            nc.scalar.activation(flip[c][:], energy[h][:, :, r0 : r0 + CHUNK], TANH)

        def quantise_z(c):
            cols = slice(c * CHUNK, (c + 1) * CHUNK)
            z_bf16 = keep.tile([P, CHUNK * PACK], BF16, name=f"z_bf16_{c}", align_bytes=64)
            nc.vector.tensor_tensor(interleaved(z_bf16[:]), by_pairs(flip[c][:]), by_pairs(gained[:, :, cols]), MULT)
            z_codes = keep.tile([P, CHUNK], U32, name=f"z_codes{c}", align_bytes=64)
            z_bytes = keep.tile([P, CHUNK], U8, name=f"z_bytes{c}", align_bytes=64)
            nc.vector.quantize_mx(out=z_codes[:].bitcast(FP8X4), scales=z_bytes[:], in_=z_bf16[:])
            z_packed[c] = (z_codes, z_bytes)

        def second_product(c):
            z_codes, z_bytes = z_packed[c]
            acc = psum.tile([P, PACK, CHUNK], F32, name=f"second{c}", tag=f"bank{c}")
            for t in range(PACK):
                product(acc[:, t, :], 1, t, z_codes[:], z_bytes[:])
            result = keep.tile([P, PACK, CHUNK], F32, name=f"result{c}", align_bytes=64)
            nc.scalar.activation(result[:], acc[:], COPY)
            nc.sync.dma_start(out=out_rows[:, :, c * CHUNK : (c + 1) * CHUNK], in_=result[:])
            result_bf16[c] = keep.tile([P, CHUNK * PACK], BF16, name=f"result_bf16_{c}", align_bytes=64)
            nc.vector.tensor_copy(interleaved(result_bf16[c][:]), by_pairs(result[:]))

        def quantise_result(c):
            cols = slice(c * CHUNK, (c + 1) * CHUNK)
            result_codes = keep.tile([P, CHUNK], I32, name=f"result_codes{c}", align_bytes=64)
            nc.vector.quantize_mx(
                out=result_codes[:].bitcast(FP8X4), scales=result_bytes[:, cols], in_=result_bf16[c][:]
            )
            nc.sync.dma_start(out=out_codes[:, cols], in_=result_codes[:])

        per_half = HALF // CHUNK
        for h in range(2):
            scalar_gathers(h)
            for k in range(LISTS):
                vector_gathers(h, k)
        energies(0)
        for h in range(2):
            gains(h)
            for c in range(h * per_half, (h + 1) * per_half):
                flips(c)
            if h == 0:
                energies(1)
            for c in range(h * per_half, (h + 1) * per_half):
                quantise_z(c)
        for c in range(S // CHUNK):
            second_product(c)
        for c in range(S // CHUNK):
            quantise_result(c)
        for q in range(QUADS):
            (nc.scalar, nc.sync)[q % 2].dma_start(
                out=out_2[0, 4 * q : 4 * q + 4, :].bitcast(I32), in_=result_bytes[32 * q : 32 * q + 4, :].bitcast(I32)
            )
